import numpy as np
import ml_dtypes


def mxq(x, axis, fmt="e4m3"):
    dtype, down = {"e4m3": (ml_dtypes.float8_e4m3fn, 7), "e5m2": (ml_dtypes.float8_e5m2, 14)}[fmt]
    v = np.moveaxis(np.asarray(x, np.float32).astype(ml_dtypes.bfloat16).astype(np.float64), axis, -1)
    blocks = v.reshape(v.shape[:-1] + (-1, 32))
    amax = np.abs(blocks).max(-1, keepdims=True)
    byte = np.maximum(np.where(amax > 0, np.frexp(amax)[1] - 1 + 127, 0) - down, 1)
    scale = np.exp2(byte - 127.0)
    codes = (blocks / scale).astype(np.float32).astype(dtype).astype(np.float64)
    return np.moveaxis((codes * scale).reshape(v.shape), -1, axis)


WIDE = False


def mx_kscale(k):
    if not WIDE:
        return np.ones(k)
    levels = np.array([30, -30])
    if k % 512:
        return np.exp2(np.random.permutation(np.resize(levels, k // 32))).repeat(32)
    a = np.empty((k // 512, 16))
    for p in range(k // 512):
        a[p, :8] = np.random.permutation(np.resize(levels, 8))
        for g in range(8):
            far = levels[np.abs(levels - a[p, g]) >= 10]
            a[p, g + 8] = far[np.random.randint(len(far))]
    return np.exp2(a.ravel()).repeat(32)


BF16 = ml_dtypes.bfloat16


def bf(x):
    return np.asarray(x, np.float32).astype(BF16)


def f64(x):
    return np.asarray(x).astype(np.float64)


N, K, Q = 1536, 1024, 512


def setup_inputs():
    s, t = mx_kscale(K), mx_kscale(Q)
    u = np.random.standard_normal((N, K)) / np.sqrt(K)
    v = np.random.standard_normal((K, N))
    w = 1 + 0.1 * np.random.standard_normal(K)
    steps = np.random.standard_normal((N, Q)) / np.sqrt(Q)
    rho = 0.5 + np.random.random(Q)
    yh = np.random.standard_t(4, (Q, N))
    return {"u": bf(u * s),
            "v": bf(v / s[:, None]),
            "w": bf(w),
            "steps": bf(steps * t),
            "rho": bf(rho),
            "yh": bf(yh / t[:, None])}


def reference(u, v, w, steps, rho, yh):
    wv = f64(w)[:, None] * f64(v)
    h = mxq(f64(u), 1, "e4m3") @ mxq(wv, 0, "e4m3")
    d = f64(rho)[:, None] * f64(yh)
    c = mxq(f64(steps), 1, "e4m3") @ mxq(d, 0, "e5m2")
    return h - c

@@ -1,0 +1,374 @@
+from contextlib import ExitStack
+
+import concourse.mybir as mybir
+from concourse.masks import make_identity
+
+N, K, Q = 1536, 1024, 512
+FLOPS = 2 * N * N * (K + Q)
+
+F32 = mybir.dt.float32
+BF16 = mybir.dt.bfloat16
+U32 = mybir.dt.uint32
+U8 = mybir.dt.uint8
+E4M3 = mybir.dt.float8_e4m3fn_x4
+E5M2 = mybir.dt.float8_e5m2_x4
+MULT = mybir.AluOpType.mult
+
+P = 128
+PACK = 4
+TILES = N // P
+PAIRS = TILES // 2
+CH = 512
+CHUNKS = N // CH
+
+
+def tile_diagonal_bfgs_left_s2_kernel(tc, u, v, w, steps, rho, yh, out):
+    nc = tc.nc
+    u_rows = u.rearrange("(p i) k -> p i k", i=TILES)
+    st_rows = steps.rearrange("(p i) k -> p i k", i=TILES)
+    out_rows = out.rearrange("(p i) n -> p i n", i=TILES)
+    v_rows = v.rearrange("(g p j) n -> g p j n", p=P, j=PACK)
+    yh_rows = yh.rearrange("(p j) n -> p j n", j=PACK)
+
+    with ExitStack() as ctx:
+        keep = ctx.enter_context(tc.tile_pool(name="keep", bufs=1))
+        work = ctx.enter_context(tc.tile_pool(name="work", bufs=3))
+        outs = ctx.enter_context(tc.tile_pool(name="outs", bufs=12))
+        psum_t = ctx.enter_context(tc.psum_pool(name="psum_t", bufs=4))
+        psum_m = ctx.enter_context(tc.psum_pool(name="psum_m", bufs=4))
+        ctx.enter_context(tc.manual_schedule())
+
+        w_sb = keep.tile([P, 2, PACK], BF16, name="w_sb")
+        rho_sb = keep.tile([P, PACK], BF16, name="rho_sb")
+        neg_rho = keep.tile([P, PACK], BF16, name="neg_rho")
+        ident = keep.tile([P, P], F32, name="ident")
+        nc.scalar.dma_start(out=w_sb[:], in_=w.rearrange("(g p j) -> p g j", p=P, j=PACK))
+        nc.scalar.dma_start(out=rho_sb[:], in_=rho.rearrange("(p j) -> p j", j=PACK))
+        make_identity(nc, ident[:])
+
+        raw = {}
+        u_raw = {}
+        st_raw = {}
+
+        def load_block(b, c0, width):
+            t = keep.tile([P, PACK, width], BF16, name="raw%d_%d" % (b, c0))
+            src = yh_rows if b == 2 else v_rows[b]
+            nc.sync.dma_start(out=t[:], in_=src[:, :, c0 * CH : c0 * CH + width])
+            for c in range(width // CH):
+                raw[b, c0 + c] = t[:, :, c * CH : (c + 1) * CH]
+
+        def load_u(i):
+            t = keep.tile([P, 2, K], BF16, name="u%d" % i)
+            nc.sync.dma_start(out=t[:], in_=u_rows[:, 2 * i : 2 * i + 2, :])
+            u_raw[i] = t
+
+        def load_st(i):
+            t = keep.tile([P, 2, Q], BF16, name="st%d" % i)
+            nc.sync.dma_start(out=t[:], in_=st_rows[:, 2 * i : 2 * i + 2, :])
+            st_raw[i] = t
+
+        scaled = {}
+        grouped = {}
+        codes = {}
+        scales = {}
+
+        def mul(b, c):
+            t = work.tile([P, PACK, CH], BF16, name="scaled")
+            for j in range(PACK):
+                factor = neg_rho[:, j : j + 1] if b == 2 else w_sb[:, b, j : j + 1]
+                nc.vector.tensor_scalar(
+                    out=t[:, j, :], in0=raw[b, c][:, j, :], scalar1=factor, scalar2=None, op0=MULT
+                )
+            scaled[b, c] = t
+
+        def interleave(b, c, engine, lo, hi):
+            if (b, c) not in grouped:
+                grouped[b, c] = work.tile([P, CH, PACK], BF16, name="grouped", align_bytes=64)
+            dst = grouped[b, c][:, lo:hi, :].rearrange("p (c i) t -> p c t i", i=4)
+            src = scaled[b, c][:, :, lo:hi].rearrange("p t (c i) -> p c t i", i=4)
+            if engine == "V":
+                nc.vector.tensor_copy(out=dst, in_=src)
+            else:
+                nc.scalar.copy(out=dst, in_=src)
+
+        def quant(b, c):
+            codes[b, c] = keep.tile([P, CH], U32, name="vc%d_%d" % (b, c), align_bytes=64)
+            scales[b, c] = keep.tile([P, CH], U8, name="vs%d_%d" % (b, c), align_bytes=64)
+            nc.vector.quantize_mx(
+                out=codes[b, c][:].bitcast(E5M2 if b == 2 else E4M3),
+                scales=scales[b, c][:],
+                in_=grouped[b, c][:].rearrange("p c t -> p (c t)"),
+            )
+
+        u_perm = {}
+        st_perm = {}
+        xt = {}
+        gu = {}
+        gs = {}
+        ucodes = {}
+        uscales = {}
+        scodes = {}
+        sscales = {}
+
+        def words_u(i, a, g, h):
+            if i in u_perm:
+                return u_perm[i][:, 2 * a + g, h, :]
+            return u_raw[i][:, a, :].bitcast(F32)[:, 256 * g + h : 256 * (g + 1) : 2]
+
+        def words_st(i, a, h):
+            if i in st_perm:
+                return st_perm[i][:, a, h, :]
+            return st_raw[i][:, a, :].bitcast(F32)[:, h:256:2]
+
+        def perm_u(i):
+            u_perm[i] = work.tile([P, 4, 2, P], F32, name="uperm", bufs=2)
+            nc.vector.tensor_copy(
+                out=u_perm[i][:],
+                in_=u_raw[i][:].rearrange("p a k -> p (a k)").bitcast(F32).rearrange("p (s r h) -> p s h r", s=4, h=2),
+            )
+
+        def perm_st(i):
+            st_perm[i] = work.tile([P, 2, 2, P], F32, name="stperm", bufs=2)
+            nc.vector.tensor_copy(
+                out=st_perm[i][:],
+                in_=st_raw[i][:].rearrange("p a k -> p (a k)").bitcast(F32).rearrange("p (s r h) -> p s h r", s=2, h=2),
+            )
+
+        def tr_u(i):
+            for a in (0, 1):
+                t = psum_t.tile([P, 4, P], F32, name="xt")
+                for g in (0, 1):
+                    for h in (0, 1):
+                        nc.tensor.transpose(t[:, 2 * g + h, :], words_u(i, a, g, h), ident[:])
+                xt[i, a] = t
+
+        def tr_st(i):
+            t = psum_t.tile([P, 4, P], F32, name="xt")
+            for a in (0, 1):
+                for h in (0, 1):
+                    nc.tensor.transpose(t[:, 2 * a + h, :], words_st(i, a, h), ident[:])
+            xt[i, 2] = t
+
+        def copy_to(engine, dst, src):
+            if engine == "V":
+                nc.vector.tensor_copy(out=dst, in_=src)
+            else:
+                nc.scalar.copy(out=dst, in_=src)
+
+        def out_u(i, a, engine):
+            if a == 0:
+                gu[i] = work.tile([P, 2, 2 * P * PACK], BF16, name="gu", align_bytes=64)
+            copy_to(
+                engine,
+                gu[i][:, a, :].bitcast(F32).rearrange("p (g r h) -> p g r h", g=2, h=2),
+                xt[i, a][:].rearrange("p (g h) r -> p g r h", h=2),
+            )
+
+        def out_st(i, engine):
+            gs[i] = work.tile([P, 2 * P * PACK], BF16, name="gs", align_bytes=64)
+            copy_to(
+                engine,
+                gs[i][:].bitcast(F32).rearrange("p (a r h) -> p a r h", a=2, h=2),
+                xt[i, 2][:].rearrange("p (a h) r -> p a r h", h=2),
+            )
+
+        def quant_u(i):
+            ucodes[i] = keep.tile([P, 4, P], U32, name="uc%d" % i, align_bytes=64)
+            uscales[i] = keep.tile([P, 4, P], U8, name="us%d" % i, align_bytes=64)
+            nc.vector.quantize_mx(
+                out=ucodes[i][:].rearrange("p s r -> p (s r)").bitcast(E4M3),
+                scales=uscales[i][:].rearrange("p s r -> p (s r)"),
+                in_=gu[i][:].rearrange("p a e -> p (a e)"),
+            )
+
+        def quant_st(i):
+            scodes[i] = keep.tile([P, 2, P], U32, name="sc%d" % i, align_bytes=64)
+            sscales[i] = keep.tile([P, 2, P], U8, name="ss%d" % i, align_bytes=64)
+            nc.vector.quantize_mx(
+                out=scodes[i][:].rearrange("p s r -> p (s r)").bitcast(E4M3),
+                scales=sscales[i][:].rearrange("p s r -> p (s r)"),
+                in_=gs[i][:],
+            )
+
+        acc = {}
+
+        def mx(i, a, c, b):
+            if b == 0:
+                acc[i, a, c] = psum_m.tile([P, CH], F32, name="acc")
+            lhs, lsc, s = (scodes[i], sscales[i], a) if b == 2 else (ucodes[i], uscales[i], 2 * a + b)
+            nc.tensor.matmul_mx(
+                out=acc[i, a, c][:],
+                lhsT=lhs[:, s, :].bitcast(E4M3),
+                lhsT_scale=lsc[:, s, :],
+                rhs=codes[b, c][:].bitcast(E5M2 if b == 2 else E4M3),
+                rhs_scale=scales[b, c][:],
+                start=(b == 0),
+                stop=(b == 2),
+            )
+
+        result = {}
+
+        def out_acc(i, a, c, engine):
+            if (i, c) not in result:
+                result[i, c] = outs.tile([P, 2, CH], F32, name="result")
+            copy_to(engine, result[i, c][:, a, :], acc[i, a, c][:])
+
+        def store(i, c):
+            nc.sync.dma_start(
+                out=out_rows[:, 2 * i : 2 * i + 2, c * CH : (c + 1) * CH], in_=result[i, c][:]
+            )
+
+        def store_tile(i, a, c):
+            nc.sync.dma_start(
+                out=out_rows[:, 2 * i + a, c * CH : (c + 1) * CH], in_=result[i, c][:, a, :]
+            )
+
+        def out_acc_half(i, a, c, h, engine):
+            if (i, c) not in result:
+                result[i, c] = outs.tile([P, 2, CH], F32, name="result")
+            copy_to(engine, result[i, c][:, a, 256 * h : 256 * (h + 1)], acc[i, a, c][:, 256 * h : 256 * (h + 1)])
+
+        def store_half(i, a, c, h):
+            nc.sync.dma_start(
+                out=out_rows[:, 2 * i + a, c * CH + 256 * h : c * CH + 256 * (h + 1)],
+                in_=result[i, c][:, a, 256 * h : 256 * (h + 1)],
+            )
+
+        load_u(0)
+        load_block(0, 0, CH)
+        load_st(0)
+        load_block(1, 0, CH)
+        load_u(1)
+        load_block(2, 0, CH)
+        load_st(1)
+        load_u(2)
+        load_st(2)
+        load_block(0, 1, CH)
+        load_u(3)
+        load_st(3)
+        load_block(1, 1, CH)
+        load_block(2, 1, CH)
+        load_u(4)
+        load_st(4)
+        load_u(5)
+        load_st(5)
+        load_block(0, 2, CH)
+        load_block(1, 2, CH)
+        load_block(2, 2, CH)
+
+        HALF = 256
+        tr_u(0)
+        out_u(0, 0, "S")
+        out_u(0, 1, "S")
+        mul(0, 0)
+        quant_u(0)
+        interleave(0, 0, "V", 0, HALF)
+        interleave(0, 0, "S", HALF, CH)
+        tr_st(0)
+        out_st(0, "S")
+        mul(1, 0)
+        quant(0, 0)
+        interleave(1, 0, "V", 0, HALF)
+        interleave(1, 0, "S", HALF, CH)
+        quant_st(0)
+        nc.vector.tensor_scalar(out=neg_rho[:], in0=rho_sb[:], scalar1=-1.0, scalar2=None, op0=MULT)
+        tr_u(1)
+        out_u(1, 0, "S")
+        out_u(1, 1, "S")
+        for a in (0, 1):
+            mx(0, a, 0, 0)
+        quant(1, 0)
+        tr_st(1)
+        mul(2, 0)
+        quant_u(1)
+        for a in (0, 1):
+            mx(0, a, 0, 1)
+        interleave(2, 0, "V", 0, HALF)
+        interleave(2, 0, "S", HALF, CH)
+        out_st(1, "S")
+        quant_st(1)
+        for a in (0, 1):
+            for b in (0, 1):
+                mx(1, a, 0, b)
+        tr_u(2)
+        quant(2, 0)
+        mul(0, 1)
+        for i in (0, 1):
+            for a in (0, 1):
+                mx(i, a, 0, 2)
+        out_u(2, 0, "S")
+        out_u(2, 1, "S")
+        tr_st(2)
+        tr_u(3)
+        out_acc(0, 0, 0, "S")
+        out_acc(0, 1, 0, "S")
+        store(0, 0)
+        out_st(2, "S")
+        quant_u(2)
+        quant_st(2)
+        interleave(0, 1, "V", 0, CH)
+        out_acc(1, 0, 0, "S")
+        out_acc(1, 1, 0, "S")
+        store(1, 0)
+        out_u(3, 0, "S")
+        out_u(3, 1, "S")
+
+        prep = []
+        order = [(0, 1), (1, 1), (2, 1), (0, 2), (1, 2), (2, 2)]
+        for n, (b, c) in enumerate(order):
+            prep.append((mul, (b, c)))
+            if n:
+                prep.append((quant, order[n - 1]))
+            prep.append((interleave, (b, c, "V", 0, CH)))
+        prep.append((quant, (2, 2)))
+        done = [2]
+
+        def do_prep(n):
+            for f, args in prep[done[0] : done[0] + n]:
+                f(*args)
+            done[0] += n
+
+        do_prep(1)
+        quant_u(3)
+        do_prep(1)
+
+        for c in range(CHUNKS):
+            for i in range(PAIRS):
+                s = c * PAIRS + i
+                last = s == CHUNKS * PAIRS - 1
+                if s < 2:
+                    continue
+                for a in (0, 1):
+                    for b in range(3):
+                        mx(i, a, c, b)
+                if s + 2 < PAIRS:
+                    tr_st(s + 1)
+                    tr_u(s + 2)
+                elif s + 1 < PAIRS:
+                    tr_st(s + 1)
+                if c == 0:
+                    if s + 1 < PAIRS:
+                        out_st(s + 1, "S")
+                        quant_st(s + 1)
+                    if s + 2 < PAIRS:
+                        out_u(s + 2, 0, "S")
+                        out_u(s + 2, 1, "S")
+                    do_prep(2)
+                    out_acc(i, 0, c, "S")
+                    out_acc(i, 1, c, "S")
+                    if s + 2 < PAIRS:
+                        quant_u(s + 2)
+                    store(i, c)
+                elif not last:
+                    busy = c == 1 and i < 3
+                    out_acc(i, 0, c, "S")
+                    out_acc(i, 1, c, "S" if busy else "V")
+                    do_prep(2 if busy else 0)
+                    store(i, c)
+                else:
+                    out_acc(i, 0, c, "S")
+                    store_tile(i, 0, c)
+                    out_acc_half(i, 1, c, 0, "V")
+                    out_acc_half(i, 1, c, 1, "S")
+                    store_half(i, 1, c, 0)
+                    store_half(i, 1, c, 1)

@@ -17,9 +17,29 @@ MULT = mybir.AluOpType.mult
 P = 128
 PACK = 4
 TILES = N // P
-PAIRS = TILES // 2
 CH = 512
-CHUNKS = N // CH
+HALF = CH // 2
+
+SCHEDULE = """
+Lu0 Lb00 Ls0 tu0 tu1 Lb10 ou0S ou1V m00 Lu1 ts0 ts1 qu0 i000S i001V Lb20 m10 os0S qu1 q00 i100S Ls1
+tu2 i101V tu3 Lu2 qs0 ou2S x0.0.0 q10 ou3S Ls2 x1.0.0 m20 x0.0.1 Lu3 qu2 i200S i201V x1.0.1 x2.0.0
+pu4 Ls3 pu5 ts2 ps4 ts3 Lb01 ps5 tu4 q20 os1S ts4 tu5 qu3 ou4S pu6 x2.0.1 Lu4 pu7 x3.0.0 ou5S ps6
+x0.0.2 ps7 x3.0.1 qs1 oa0.0S x1.0.2 qu4 Ls4 x2.0.2 qu5 oa1.0S x3.0.2 m01 Lb11 ts5 oa2.0S tu6 oa3.0V
+ts6 os2S pu8 pu9 ou6S Lb21 ps8 tu7 ps9 qs2 ts7 ou7S x4.0.0 os3V tu8 Ls5 qu6 ts9 ts8 qu7 ou8S x4.0.1
+Lu5 qs3 os4S tu9 qu8 x4.0.2 m11 ou9S x5.0.0 Lb02 x6.0.0 oa4.0S qs4 x5.0.1 qu9 x6.0.1 ps10 x5.0.2
+ps11 i010V x6.0.2 Lb12 oa5.0S ts10 i011V ts11 oa6.0S x7.0.0 x8.0.0 pu10 os5S x7.0.1 pu11 Lb22 x8.0.1
+m21 tu10 i110V tu11 ou10S WP0.0 x7.0.2 i111V x8.0.2 ou11S x9.0.0 qu10 x9.0.1 oa7.0S x9.0.2 qu11
+WP1.0 x10.0.0 oa8.0S q01 x11.0.0 oa9.0S x10.0.1 i210V x11.0.1 WP2.0 x0.1.0 i211V x1.1.0 qs5 q11
+WP3.0 x10.0.2 x11.0.2 q21 oa10.0S x0.1.1 x1.1.1 oa11.0V WP4.0 x0.1.2 m02 x1.1.2 oa0.1S x2.1.0 x3.1.0
+oa1.1V x2.1.1 WP5.0 x3.1.1 m12 x2.1.2 x3.1.2 i020V oa2.1S x4.1.0 WP0.1 x5.1.0 i021V oa3.1S x4.1.1
+x5.1.1 m22 x4.1.2 x5.1.2 i120V oa4.1S x6.1.0 x7.1.0 WP1.1 oa5.1S x6.1.1 i121V x7.1.1 x6.1.2 q02
+x7.1.2 oa6.1S x8.1.0 i220V x9.1.0 WP2.1 oa7.1S x8.1.1 i221V x9.1.1 x8.1.2 q12 x9.1.2 oa8.1S x10.1.0
+q22 x11.1.0 WP3.1 oa9.1S x10.1.1 x11.1.1 x10.1.2 x11.1.2 oa10.1S x0.2.0 oa11.1V x0.2.1 WP4.1 x0.2.2
+x1.2.0 x1.2.1 x1.2.2 oa0.2S x2.2.0 WP5.1 oa1.2V x2.2.1 x2.2.2 x3.2.0 x3.2.1 x3.2.2 oa2.2S x4.2.0
+WP0.2 oa3.2V x4.2.1 x4.2.2 x5.2.0 x5.2.1 x5.2.2 oa4.2S x6.2.0 WP1.2 oa5.2V x6.2.1 x6.2.2 x7.2.0
+x7.2.1 x7.2.2 oa6.2S x8.2.0 WP2.2 oa7.2V x8.2.1 x8.2.2 x9.2.0 x9.2.1 x9.2.2 oa8.2S x10.2.0 WP3.2
+oa9.2V x10.2.1 x10.2.2 x11.2.0 x11.2.1 x11.2.2 oa10.2S WP4.2 oa11.2V W10.2 W11.2
+"""
 
 
 def tile_diagonal_bfgs_left_s2_kernel(tc, u, v, w, steps, rho, yh, out):
@@ -46,34 +66,100 @@ def tile_diagonal_bfgs_left_s2_kernel(tc, u, v, w, steps, rho, yh, out):
         nc.scalar.dma_start(out=rho_sb[:], in_=rho.rearrange("(p j) -> p j", j=PACK))
         make_identity(nc, ident[:])
 
-        raw = {}
-        u_raw = {}
-        st_raw = {}
+        raw, u_raw, st_raw, words_u, words_st = {}, {}, {}, {}, {}
+        scaled, grouped, codes, scales = {}, {}, {}, {}
+        xt, gu, gs, ucodes, uscales, scodes, sscales = {}, {}, {}, {}, {}, {}, {}
+        acc, result = {}, {}
 
-        def load_block(b, c0, width):
-            t = keep.tile([P, PACK, width], BF16, name="raw%d_%d" % (b, c0))
-            src = yh_rows if b == 2 else v_rows[b]
-            nc.sync.dma_start(out=t[:], in_=src[:, :, c0 * CH : c0 * CH + width])
-            for c in range(width // CH):
-                raw[b, c0 + c] = t[:, :, c * CH : (c + 1) * CH]
+        def copy_to(engine, dst, src):
+            if engine == "V":
+                nc.vector.tensor_copy(out=dst, in_=src)
+            else:
+                nc.scalar.copy(out=dst, in_=src)
 
-        def load_u(i):
-            t = keep.tile([P, 2, K], BF16, name="u%d" % i)
-            nc.sync.dma_start(out=t[:], in_=u_rows[:, 2 * i : 2 * i + 2, :])
-            u_raw[i] = t
+        def load(kind, arg):
+            if kind == "u":
+                i = int(arg)
+                t = keep.tile([P, 2, K], BF16, name="u%d" % i)
+                nc.sync.dma_start(out=t[:], in_=u_rows[:, 2 * i : 2 * i + 2, :])
+                for a in (0, 1):
+                    u_raw[2 * i + a] = t[:, a, :].bitcast(F32)
+            elif kind == "s":
+                i = int(arg)
+                t = keep.tile([P, 2, Q], BF16, name="st%d" % i)
+                nc.sync.dma_start(out=t[:], in_=st_rows[:, 2 * i : 2 * i + 2, :])
+                for a in (0, 1):
+                    st_raw[2 * i + a] = t[:, a, :].bitcast(F32)
+            else:
+                b, c = int(arg[0]), int(arg[1:] or 1)
+                width = CH if kind == "b" else 2 * CH
+                t = keep.tile([P, PACK, width], BF16, name="raw%d_%d" % (b, c))
+                src = yh_rows if b == 2 else v_rows[b]
+                nc.sync.dma_start(out=t[:], in_=src[:, :, c * CH : c * CH + width])
+                for d in range(width // CH):
+                    raw[b, c + d] = t[:, :, d * CH : (d + 1) * CH]
 
-        def load_st(i):
-            t = keep.tile([P, 2, Q], BF16, name="st%d" % i)
-            nc.sync.dma_start(out=t[:], in_=st_rows[:, 2 * i : 2 * i + 2, :])
-            st_raw[i] = t
+        def perm_u(t):
+            x = work.tile([P, 2, 2, P], F32, name="uperm", bufs=3)
+            nc.vector.tensor_copy(out=x[:], in_=u_raw[t].rearrange("p (g r h) -> p g h r", g=2, h=2))
+            words_u[t] = x
 
-        scaled = {}
-        grouped = {}
-        codes = {}
-        scales = {}
+        def perm_s(t):
+            x = work.tile([P, 2, P], F32, name="sperm", bufs=3)
+            nc.vector.tensor_copy(out=x[:], in_=st_raw[t].rearrange("p (r h) -> p h r", h=2))
+            words_st[t] = x
+
+        def tr_u(t):
+            x = psum_t.tile([P, 4, P], F32, name="xt")
+            for g in (0, 1):
+                for h in (0, 1):
+                    if t in words_u:
+                        src = words_u[t][:, g, h, :]
+                    else:
+                        src = u_raw[t][:, 256 * g + h : 256 * (g + 1) : 2]
+                    nc.tensor.transpose(x[:, 2 * g + h, :], src, ident[:])
+            xt["u", t] = x
+
+        def tr_s(t):
+            i, a = divmod(t, 2)
+            if ("s", i) not in xt:
+                xt["s", i] = psum_t.tile([P, 4, P], F32, name="xt")
+            for h in (0, 1):
+                src = words_st[t][:, h, :] if t in words_st else st_raw[t][:, h:256:2]
+                nc.tensor.transpose(xt["s", i][:, 2 * a + h, :], src, ident[:])
+
+        def out_u(t, engine):
+            gu[t] = work.tile([P, 2 * P * PACK], BF16, name="gu", align_bytes=64, bufs=4)
+            copy_to(
+                engine,
+                gu[t][:].bitcast(F32).rearrange("p (g r h) -> p g r h", g=2, h=2),
+                xt["u", t][:].rearrange("p (g h) r -> p g r h", h=2),
+            )
+
+        def out_s(i, engine):
+            gs[i] = work.tile([P, 2 * P * PACK], BF16, name="gs", align_bytes=64)
+            copy_to(
+                engine,
+                gs[i][:].bitcast(F32).rearrange("p (a r h) -> p a r h", a=2, h=2),
+                xt["s", i][:].rearrange("p (a h) r -> p a r h", h=2),
+            )
+
+        def quant_u(t):
+            ucodes[t] = keep.tile([P, 2 * P], U32, name="uc%d" % t, align_bytes=64)
+            uscales[t] = keep.tile([P, 2 * P], U8, name="us%d" % t, align_bytes=64)
+            nc.vector.quantize_mx(out=ucodes[t][:].bitcast(E4M3), scales=uscales[t][:], in_=gu[t][:])
+
+        def quant_s(i):
+            scodes[i] = keep.tile([P, 2 * P], U32, name="sc%d" % i, align_bytes=64)
+            sscales[i] = keep.tile([P, 2 * P], U8, name="ss%d" % i, align_bytes=64)
+            nc.vector.quantize_mx(out=scodes[i][:].bitcast(E4M3), scales=sscales[i][:], in_=gs[i][:])
 
         def mul(b, c):
-            t = work.tile([P, PACK, CH], BF16, name="scaled")
+            if b == 2 and c == 0:
+                nc.vector.tensor_scalar(
+                    out=neg_rho[:], in0=rho_sb[:], scalar1=-1.0, scalar2=None, op0=MULT
+                )
+            t = work.tile([P, PACK, CH], BF16, name="scaled", bufs=4)
             for j in range(PACK):
                 factor = neg_rho[:, j : j + 1] if b == 2 else w_sb[:, b, j : j + 1]
                 nc.vector.tensor_scalar(
@@ -81,15 +167,15 @@ def tile_diagonal_bfgs_left_s2_kernel(tc, u, v, w, steps, rho, yh, out):
                 )
             scaled[b, c] = t
 
-        def interleave(b, c, engine, lo, hi):
+        def interleave(b, c, h, engine):
             if (b, c) not in grouped:
-                grouped[b, c] = work.tile([P, CH, PACK], BF16, name="grouped", align_bytes=64)
-            dst = grouped[b, c][:, lo:hi, :].rearrange("p (c i) t -> p c t i", i=4)
-            src = scaled[b, c][:, :, lo:hi].rearrange("p t (c i) -> p c t i", i=4)
-            if engine == "V":
-                nc.vector.tensor_copy(out=dst, in_=src)
-            else:
-                nc.scalar.copy(out=dst, in_=src)
+                grouped[b, c] = work.tile([P, CH, PACK], BF16, name="grouped", align_bytes=64, bufs=4)
+            cols = slice(HALF * h, HALF * (h + 1))
+            copy_to(
+                engine,
+                grouped[b, c][:, cols, :].rearrange("p (c i) t -> p c t i", i=4),
+                scaled[b, c][:, :, cols].rearrange("p t (c i) -> p c t i", i=4),
+            )
 
         def quant(b, c):
             codes[b, c] = keep.tile([P, CH], U32, name="vc%d_%d" % (b, c), align_bytes=64)
@@ -100,275 +186,81 @@ def tile_diagonal_bfgs_left_s2_kernel(tc, u, v, w, steps, rho, yh, out):
                 in_=grouped[b, c][:].rearrange("p c t -> p (c t)"),
             )
 
-        u_perm = {}
-        st_perm = {}
-        xt = {}
-        gu = {}
-        gs = {}
-        ucodes = {}
-        uscales = {}
-        scodes = {}
-        sscales = {}
-
-        def words_u(i, a, g, h):
-            if i in u_perm:
-                return u_perm[i][:, 2 * a + g, h, :]
-            return u_raw[i][:, a, :].bitcast(F32)[:, 256 * g + h : 256 * (g + 1) : 2]
-
-        def words_st(i, a, h):
-            if i in st_perm:
-                return st_perm[i][:, a, h, :]
-            return st_raw[i][:, a, :].bitcast(F32)[:, h:256:2]
-
-        def perm_u(i):
-            u_perm[i] = work.tile([P, 4, 2, P], F32, name="uperm", bufs=2)
-            nc.vector.tensor_copy(
-                out=u_perm[i][:],
-                in_=u_raw[i][:].rearrange("p a k -> p (a k)").bitcast(F32).rearrange("p (s r h) -> p s h r", s=4, h=2),
-            )
-
-        def perm_st(i):
-            st_perm[i] = work.tile([P, 2, 2, P], F32, name="stperm", bufs=2)
-            nc.vector.tensor_copy(
-                out=st_perm[i][:],
-                in_=st_raw[i][:].rearrange("p a k -> p (a k)").bitcast(F32).rearrange("p (s r h) -> p s h r", s=2, h=2),
-            )
-
-        def tr_u(i):
-            for a in (0, 1):
-                t = psum_t.tile([P, 4, P], F32, name="xt")
-                for g in (0, 1):
-                    for h in (0, 1):
-                        nc.tensor.transpose(t[:, 2 * g + h, :], words_u(i, a, g, h), ident[:])
-                xt[i, a] = t
-
-        def tr_st(i):
-            t = psum_t.tile([P, 4, P], F32, name="xt")
-            for a in (0, 1):
-                for h in (0, 1):
-                    nc.tensor.transpose(t[:, 2 * a + h, :], words_st(i, a, h), ident[:])
-            xt[i, 2] = t
-
-        def copy_to(engine, dst, src):
-            if engine == "V":
-                nc.vector.tensor_copy(out=dst, in_=src)
-            else:
-                nc.scalar.copy(out=dst, in_=src)
-
-        def out_u(i, a, engine):
-            if a == 0:
-                gu[i] = work.tile([P, 2, 2 * P * PACK], BF16, name="gu", align_bytes=64)
-            copy_to(
-                engine,
-                gu[i][:, a, :].bitcast(F32).rearrange("p (g r h) -> p g r h", g=2, h=2),
-                xt[i, a][:].rearrange("p (g h) r -> p g r h", h=2),
-            )
-
-        def out_st(i, engine):
-            gs[i] = work.tile([P, 2 * P * PACK], BF16, name="gs", align_bytes=64)
-            copy_to(
-                engine,
-                gs[i][:].bitcast(F32).rearrange("p (a r h) -> p a r h", a=2, h=2),
-                xt[i, 2][:].rearrange("p (a h) r -> p a r h", h=2),
-            )
-
-        def quant_u(i):
-            ucodes[i] = keep.tile([P, 4, P], U32, name="uc%d" % i, align_bytes=64)
-            uscales[i] = keep.tile([P, 4, P], U8, name="us%d" % i, align_bytes=64)
-            nc.vector.quantize_mx(
-                out=ucodes[i][:].rearrange("p s r -> p (s r)").bitcast(E4M3),
-                scales=uscales[i][:].rearrange("p s r -> p (s r)"),
-                in_=gu[i][:].rearrange("p a e -> p (a e)"),
-            )
-
-        def quant_st(i):
-            scodes[i] = keep.tile([P, 2, P], U32, name="sc%d" % i, align_bytes=64)
-            sscales[i] = keep.tile([P, 2, P], U8, name="ss%d" % i, align_bytes=64)
-            nc.vector.quantize_mx(
-                out=scodes[i][:].rearrange("p s r -> p (s r)").bitcast(E4M3),
-                scales=sscales[i][:].rearrange("p s r -> p (s r)"),
-                in_=gs[i][:],
-            )
-
-        acc = {}
-
-        def mx(i, a, c, b):
+        def mx(t, c, b):
             if b == 0:
-                acc[i, a, c] = psum_m.tile([P, CH], F32, name="acc")
-            lhs, lsc, s = (scodes[i], sscales[i], a) if b == 2 else (ucodes[i], uscales[i], 2 * a + b)
+                acc[t, c] = psum_m.tile([P, CH], F32, name="acc")
+            if b == 2:
+                i, s = divmod(t, 2)
+                lhs, lsc = scodes[i], sscales[i]
+            else:
+                lhs, lsc, s = ucodes[t], uscales[t], b
             nc.tensor.matmul_mx(
-                out=acc[i, a, c][:],
-                lhsT=lhs[:, s, :].bitcast(E4M3),
-                lhsT_scale=lsc[:, s, :],
+                out=acc[t, c][:],
+                lhsT=lhs[:, s * P : (s + 1) * P].bitcast(E4M3),
+                lhsT_scale=lsc[:, s * P : (s + 1) * P],
                 rhs=codes[b, c][:].bitcast(E5M2 if b == 2 else E4M3),
                 rhs_scale=scales[b, c][:],
                 start=(b == 0),
                 stop=(b == 2),
             )
 
-        result = {}
+        def result_of(t, c):
+            if (t // 2, c) not in result:
+                result[t // 2, c] = outs.tile([P, 2, CH], F32, name="result")
+            return result[t // 2, c][:, t % 2, :]
 
-        def out_acc(i, a, c, engine):
-            if (i, c) not in result:
-                result[i, c] = outs.tile([P, 2, CH], F32, name="result")
-            copy_to(engine, result[i, c][:, a, :], acc[i, a, c][:])
+        def out_acc(t, c, engine):
+            dst = result_of(t, c)
+            if (t, c) == LAST:
+                for h, e in ((0, "V"), (1, "S")):
+                    cols = slice(HALF * h, HALF * (h + 1))
+                    copy_to(e, dst[:, cols], acc[t, c][:, cols])
+            else:
+                copy_to(engine, dst, acc[t, c][:])
 
-        def store(i, c):
+        def store(t, c):
+            for cols in (slice(0, HALF), slice(HALF, CH)) if (t, c) == LAST else (slice(0, CH),):
+                nc.sync.dma_start(
+                    out=out_rows[:, t, c * CH + cols.start : c * CH + cols.stop], in_=result_of(t, c)[:, cols]
+                )
+
+        def store_pair(i, c):
             nc.sync.dma_start(
                 out=out_rows[:, 2 * i : 2 * i + 2, c * CH : (c + 1) * CH], in_=result[i, c][:]
             )
 
-        def store_tile(i, a, c):
-            nc.sync.dma_start(
-                out=out_rows[:, 2 * i + a, c * CH : (c + 1) * CH], in_=result[i, c][:, a, :]
-            )
-
-        def out_acc_half(i, a, c, h, engine):
-            if (i, c) not in result:
-                result[i, c] = outs.tile([P, 2, CH], F32, name="result")
-            copy_to(engine, result[i, c][:, a, 256 * h : 256 * (h + 1)], acc[i, a, c][:, 256 * h : 256 * (h + 1)])
-
-        def store_half(i, a, c, h):
-            nc.sync.dma_start(
-                out=out_rows[:, 2 * i + a, c * CH + 256 * h : c * CH + 256 * (h + 1)],
-                in_=result[i, c][:, a, 256 * h : 256 * (h + 1)],
-            )
-
-        load_u(0)
-        load_block(0, 0, CH)
-        load_st(0)
-        load_block(1, 0, CH)
-        load_u(1)
-        load_block(2, 0, CH)
-        load_st(1)
-        load_u(2)
-        load_st(2)
-        load_block(0, 1, CH)
-        load_u(3)
-        load_st(3)
-        load_block(1, 1, CH)
-        load_block(2, 1, CH)
-        load_u(4)
-        load_st(4)
-        load_u(5)
-        load_st(5)
-        load_block(0, 2, CH)
-        load_block(1, 2, CH)
-        load_block(2, 2, CH)
-
-        HALF = 256
-        tr_u(0)
-        out_u(0, 0, "S")
-        out_u(0, 1, "S")
-        mul(0, 0)
-        quant_u(0)
-        interleave(0, 0, "V", 0, HALF)
-        interleave(0, 0, "S", HALF, CH)
-        tr_st(0)
-        out_st(0, "S")
-        mul(1, 0)
-        quant(0, 0)
-        interleave(1, 0, "V", 0, HALF)
-        interleave(1, 0, "S", HALF, CH)
-        quant_st(0)
-        nc.vector.tensor_scalar(out=neg_rho[:], in0=rho_sb[:], scalar1=-1.0, scalar2=None, op0=MULT)
-        tr_u(1)
-        out_u(1, 0, "S")
-        out_u(1, 1, "S")
-        for a in (0, 1):
-            mx(0, a, 0, 0)
-        quant(1, 0)
-        tr_st(1)
-        mul(2, 0)
-        quant_u(1)
-        for a in (0, 1):
-            mx(0, a, 0, 1)
-        interleave(2, 0, "V", 0, HALF)
-        interleave(2, 0, "S", HALF, CH)
-        out_st(1, "S")
-        quant_st(1)
-        for a in (0, 1):
-            for b in (0, 1):
-                mx(1, a, 0, b)
-        tr_u(2)
-        quant(2, 0)
-        mul(0, 1)
-        for i in (0, 1):
-            for a in (0, 1):
-                mx(i, a, 0, 2)
-        out_u(2, 0, "S")
-        out_u(2, 1, "S")
-        tr_st(2)
-        tr_u(3)
-        out_acc(0, 0, 0, "S")
-        out_acc(0, 1, 0, "S")
-        store(0, 0)
-        out_st(2, "S")
-        quant_u(2)
-        quant_st(2)
-        interleave(0, 1, "V", 0, CH)
-        out_acc(1, 0, 0, "S")
-        out_acc(1, 1, 0, "S")
-        store(1, 0)
-        out_u(3, 0, "S")
-        out_u(3, 1, "S")
-
-        prep = []
-        order = [(0, 1), (1, 1), (2, 1), (0, 2), (1, 2), (2, 2)]
-        for n, (b, c) in enumerate(order):
-            prep.append((mul, (b, c)))
-            if n:
-                prep.append((quant, order[n - 1]))
-            prep.append((interleave, (b, c, "V", 0, CH)))
-        prep.append((quant, (2, 2)))
-        done = [2]
-
-        def do_prep(n):
-            for f, args in prep[done[0] : done[0] + n]:
-                f(*args)
-            done[0] += n
-
-        do_prep(1)
-        quant_u(3)
-        do_prep(1)
-
-        for c in range(CHUNKS):
-            for i in range(PAIRS):
-                s = c * PAIRS + i
-                last = s == CHUNKS * PAIRS - 1
-                if s < 2:
-                    continue
-                for a in (0, 1):
-                    for b in range(3):
-                        mx(i, a, c, b)
-                if s + 2 < PAIRS:
-                    tr_st(s + 1)
-                    tr_u(s + 2)
-                elif s + 1 < PAIRS:
-                    tr_st(s + 1)
-                if c == 0:
-                    if s + 1 < PAIRS:
-                        out_st(s + 1, "S")
-                        quant_st(s + 1)
-                    if s + 2 < PAIRS:
-                        out_u(s + 2, 0, "S")
-                        out_u(s + 2, 1, "S")
-                    do_prep(2)
-                    out_acc(i, 0, c, "S")
-                    out_acc(i, 1, c, "S")
-                    if s + 2 < PAIRS:
-                        quant_u(s + 2)
-                    store(i, c)
-                elif not last:
-                    busy = c == 1 and i < 3
-                    out_acc(i, 0, c, "S")
-                    out_acc(i, 1, c, "S" if busy else "V")
-                    do_prep(2 if busy else 0)
-                    store(i, c)
-                else:
-                    out_acc(i, 0, c, "S")
-                    store_tile(i, 0, c)
-                    out_acc_half(i, 1, c, 0, "V")
-                    out_acc_half(i, 1, c, 1, "S")
-                    store_half(i, 1, c, 0)
-                    store_half(i, 1, c, 1)
+        LAST = (11, 2)
+        for step in SCHEDULE.split():
+            if step[:1] == "L":
+                load(step[1:2], step[2:])
+            elif step[:2] == "WP":
+                store_pair(*[int(x) for x in step[2:].split(".")])
+            elif step[:1] == "W":
+                store(*[int(x) for x in step[1:].split(".")])
+            elif step[:2] == "pu":
+                perm_u(int(step[2:]))
+            elif step[:2] == "ps":
+                perm_s(int(step[2:]))
+            elif step[:2] == "tu":
+                tr_u(int(step[2:]))
+            elif step[:2] == "ts":
+                tr_s(int(step[2:]))
+            elif step[:2] == "ou":
+                out_u(int(step[2:-1]), step[-1:])
+            elif step[:2] == "os":
+                out_s(int(step[2:-1]), step[-1:])
+            elif step[:2] == "qu":
+                quant_u(int(step[2:]))
+            elif step[:2] == "qs":
+                quant_s(int(step[2:]))
+            elif step[:1] == "m":
+                mul(int(step[1:2]), int(step[2:]))
+            elif step[:1] == "i":
+                interleave(int(step[1:2]), int(step[2:3]), int(step[3:4]), step[4:])
+            elif step[:1] == "q":
+                quant(int(step[1:2]), int(step[2:]))
+            elif step[:1] == "x":
+                mx(*[int(x) for x in step[1:].split(".")])
+            else:
+                t, c = step[2:-1].split(".")
+                out_acc(int(t), int(c), step[-1:])

@@ -21,24 +21,24 @@ CH = 512
 HALF = CH // 2
 
 SCHEDULE = """
-Lu0 Lb00 Ls0 tu0 tu1 Lb10 ou0S ou1V m00 Lu1 ts0 ts1 qu0 i000S i001V Lb20 m10 os0S qu1 q00 i100S Ls1
-tu2 i101V tu3 Lu2 qs0 ou2S x0.0.0 q10 ou3S Ls2 x1.0.0 m20 x0.0.1 Lu3 qu2 i200S i201V x1.0.1 x2.0.0
-pu4 Ls3 pu5 ts2 ps4 ts3 Lb01 ps5 tu4 q20 os1S ts4 tu5 qu3 ou4S pu6 x2.0.1 Lu4 pu7 x3.0.0 ou5S ps6
-x0.0.2 ps7 x3.0.1 qs1 oa0.0S x1.0.2 qu4 Ls4 x2.0.2 qu5 oa1.0S x3.0.2 m01 Lb11 ts5 oa2.0S tu6 oa3.0V
-ts6 os2S pu8 pu9 ou6S Lb21 ps8 tu7 ps9 qs2 ts7 ou7S x4.0.0 os3V tu8 Ls5 qu6 ts9 ts8 qu7 ou8S x4.0.1
-Lu5 qs3 os4S tu9 qu8 x4.0.2 m11 ou9S x5.0.0 Lb02 x6.0.0 oa4.0S qs4 x5.0.1 qu9 x6.0.1 ps10 x5.0.2
-ps11 i010V x6.0.2 Lb12 oa5.0S ts10 i011V ts11 oa6.0S x7.0.0 x8.0.0 pu10 os5S x7.0.1 pu11 Lb22 x8.0.1
-m21 tu10 i110V tu11 ou10S WP0.0 x7.0.2 i111V x8.0.2 ou11S x9.0.0 qu10 x9.0.1 oa7.0S x9.0.2 qu11
-WP1.0 x10.0.0 oa8.0S q01 x11.0.0 oa9.0S x10.0.1 i210V x11.0.1 WP2.0 x0.1.0 i211V x1.1.0 qs5 q11
-WP3.0 x10.0.2 x11.0.2 q21 oa10.0S x0.1.1 x1.1.1 oa11.0V WP4.0 x0.1.2 m02 x1.1.2 oa0.1S x2.1.0 x3.1.0
-oa1.1V x2.1.1 WP5.0 x3.1.1 m12 x2.1.2 x3.1.2 i020V oa2.1S x4.1.0 WP0.1 x5.1.0 i021V oa3.1S x4.1.1
-x5.1.1 m22 x4.1.2 x5.1.2 i120V oa4.1S x6.1.0 x7.1.0 WP1.1 oa5.1S x6.1.1 i121V x7.1.1 x6.1.2 q02
-x7.1.2 oa6.1S x8.1.0 i220V x9.1.0 WP2.1 oa7.1S x8.1.1 i221V x9.1.1 x8.1.2 q12 x9.1.2 oa8.1S x10.1.0
-q22 x11.1.0 WP3.1 oa9.1S x10.1.1 x11.1.1 x10.1.2 x11.1.2 oa10.1S x0.2.0 oa11.1V x0.2.1 WP4.1 x0.2.2
-x1.2.0 x1.2.1 x1.2.2 oa0.2S x2.2.0 WP5.1 oa1.2V x2.2.1 x2.2.2 x3.2.0 x3.2.1 x3.2.2 oa2.2S x4.2.0
-WP0.2 oa3.2V x4.2.1 x4.2.2 x5.2.0 x5.2.1 x5.2.2 oa4.2S x6.2.0 WP1.2 oa5.2V x6.2.1 x6.2.2 x7.2.0
-x7.2.1 x7.2.2 oa6.2S x8.2.0 WP2.2 oa7.2V x8.2.1 x8.2.2 x9.2.0 x9.2.1 x9.2.2 oa8.2S x10.2.0 WP3.2
-oa9.2V x10.2.1 x10.2.2 x11.2.0 x11.2.1 x11.2.2 oa10.2S WP4.2 oa11.2V W10.2 W11.2
+Lu0 Lb00 Lu1 tu0 tu1 ou0S Ls0 m00 ou1S Lu2 qu0 i001S i000V tu2 Lb20 qu1 tu3 ou2V ts0 ts1 ou3S q00
+Lb10 tu4 os0S qu2 qu3 tu5 ou4S qs0 Lu3 x2.0.0 m20 ou5S x3.0.0 qu4 i201S Ls1 i200V x0.0.0 Ls3 qu5
+x4.0.0 m10 Ls2 q20 tu6 i101S Lb11 ts2 i100V ts3 tu7 ou6V os1S Lu4 ts6 q10 ts7 ou7S ts4 qs1 ts5 os3S
+qu6 Ls5 x2.0.1 qu7 os2S x3.0.1 m11 x2.0.2 Ls4 x3.0.2 qs3 oa2.0S x4.0.1 Lu5 qs2 x0.0.1 pu8 i110S
+x0.0.2 pu9 x6.0.0 ps10 ps11 Lb01 tu8 i111V tu9 oa3.0S ts10 ou8V ts11 oa0.0S x6.0.1 Lb02 ou9V x7.0.0
+os5S x6.0.2 qu8 x7.0.1 qu9 oa6.0S x4.0.2 Lb22 qs5 x7.0.2 ps8 oa4.0S x5.0.0 ps9 pu10 ts8 oa7.0S pu11
+ts9 tu10 q11 Lb21 os4S tu11 m01 x5.0.1 ou10S x8.0.0 qs4 Lb12 x5.0.2 ou11S i010V x8.0.1 i011S x9.0.0
+qu10 x8.0.2 qu11 x9.0.1 WP1.0 oa5.0V x10.0.0 oa8.0S x9.0.2 m21 x10.0.1 oa9.0S x11.0.0 WP3.0 q01
+x10.0.2 i210S x11.0.1 x1.0.0 i211V x11.0.2 WP2.0 x1.0.1 oa10.0V x0.1.0 oa11.0S x1.0.2 q21 x0.1.1
+WP4.0 oa1.0S x1.1.0 m22 x2.1.0 x0.1.2 m12 x1.1.1 WP5.0 oa0.1S x2.1.1 i220V x1.1.2 x2.1.2 i221V
+oa1.1S x3.1.0 WP0.0 x4.1.0 oa2.1S x3.1.1 i120V x4.1.1 x3.1.2 q22 x4.1.2 WP0.1 oa3.1S x5.1.0 i121V
+x6.1.0 oa4.1S x5.1.1 m02 x6.1.1 x5.1.2 q12 x6.1.2 WP1.1 oa5.1S x7.1.0 i020V x8.1.0 oa6.1S x7.1.1
+x8.1.1 i021V x7.1.2 x8.1.2 WP2.1 oa7.1S q02 x9.1.0 x10.1.0 oa8.1S x9.1.1 x10.1.1 x9.1.2 x10.1.2
+WP3.1 oa9.1S x11.1.0 oa10.1V x0.2.0 x11.1.1 x0.2.1 x11.1.2 x0.2.2 WP4.1 oa11.1S x1.2.0 oa0.2V x1.2.1
+x1.2.2 x2.2.0 oa1.2S x2.2.1 x2.2.2 WP5.1 x3.2.0 oa2.2V x3.2.1 x3.2.2 x4.2.0 WP0.2 oa3.2S x4.2.1
+x4.2.2 x5.2.0 oa4.2V x5.2.1 x5.2.2 x6.2.0 WP1.2 oa5.2S x6.2.1 x6.2.2 x7.2.0 oa6.2V x7.2.1 x7.2.2
+x8.2.0 WP2.2 oa7.2S x8.2.1 x8.2.2 x9.2.0 oa8.2V x9.2.1 x9.2.2 x10.2.0 WP3.2 oa9.2S x10.2.1 x10.2.2
+x11.2.0 oa10.2V x11.2.1 x11.2.2 WP4.2 oa11.2S W10.2 W11.2
 """
 
 

@@ -16,251 +16,302 @@ MULT = mybir.AluOpType.mult
 
 P = 128
 PACK = 4
+PAIRS_PASS = 2 * P
 TILES = N // P
-CH = 512
-HALF = CH // 2
+CHUNK = 512
+HALF = CHUNK // 2
 
-SCHEDULE = """
-Lu0 Lb00 Lu1 tu0 tu1 ou0S Ls0 m00 ou1S Lu2 qu0 i001S i000V tu2 Lb20 qu1 tu3 ou2V ts0 ts1 ou3S q00
-Lb10 tu4 os0S qu2 qu3 tu5 ou4S qs0 Lu3 x2.0.0 m20 ou5S x3.0.0 qu4 i201S Ls1 i200V x0.0.0 Ls3 qu5
-x4.0.0 m10 Ls2 q20 tu6 i101S Lb11 ts2 i100V ts3 tu7 ou6V os1S Lu4 ts6 q10 ts7 ou7S ts4 qs1 ts5 os3S
-qu6 Ls5 x2.0.1 qu7 os2S x3.0.1 m11 x2.0.2 Ls4 x3.0.2 qs3 oa2.0S x4.0.1 Lu5 qs2 x0.0.1 pu8 i110S
-x0.0.2 pu9 x6.0.0 ps10 ps11 Lb01 tu8 i111V tu9 oa3.0S ts10 ou8V ts11 oa0.0S x6.0.1 Lb02 ou9V x7.0.0
-os5S x6.0.2 qu8 x7.0.1 qu9 oa6.0S x4.0.2 Lb22 qs5 x7.0.2 ps8 oa4.0S x5.0.0 ps9 pu10 ts8 oa7.0S pu11
-ts9 tu10 q11 Lb21 os4S tu11 m01 x5.0.1 ou10S x8.0.0 qs4 Lb12 x5.0.2 ou11S i010V x8.0.1 i011S x9.0.0
-qu10 x8.0.2 qu11 x9.0.1 WP1.0 oa5.0V x10.0.0 oa8.0S x9.0.2 m21 x10.0.1 oa9.0S x11.0.0 WP3.0 q01
-x10.0.2 i210S x11.0.1 x1.0.0 i211V x11.0.2 WP2.0 x1.0.1 oa10.0V x0.1.0 oa11.0S x1.0.2 q21 x0.1.1
-WP4.0 oa1.0S x1.1.0 m22 x2.1.0 x0.1.2 m12 x1.1.1 WP5.0 oa0.1S x2.1.1 i220V x1.1.2 x2.1.2 i221V
-oa1.1S x3.1.0 WP0.0 x4.1.0 oa2.1S x3.1.1 i120V x4.1.1 x3.1.2 q22 x4.1.2 WP0.1 oa3.1S x5.1.0 i121V
-x6.1.0 oa4.1S x5.1.1 m02 x6.1.1 x5.1.2 q12 x6.1.2 WP1.1 oa5.1S x7.1.0 i020V x8.1.0 oa6.1S x7.1.1
-x8.1.1 i021V x7.1.2 x8.1.2 WP2.1 oa7.1S q02 x9.1.0 x10.1.0 oa8.1S x9.1.1 x10.1.1 x9.1.2 x10.1.2
-WP3.1 oa9.1S x11.1.0 oa10.1V x0.2.0 x11.1.1 x0.2.1 x11.1.2 x0.2.2 WP4.1 oa11.1S x1.2.0 oa0.2V x1.2.1
-x1.2.2 x2.2.0 oa1.2S x2.2.1 x2.2.2 WP5.1 x3.2.0 oa2.2V x3.2.1 x3.2.2 x4.2.0 WP0.2 oa3.2S x4.2.1
-x4.2.2 x5.2.0 oa4.2V x5.2.1 x5.2.2 x6.2.0 WP1.2 oa5.2S x6.2.1 x6.2.2 x7.2.0 oa6.2V x7.2.1 x7.2.2
-x8.2.0 WP2.2 oa7.2S x8.2.1 x8.2.2 x9.2.0 oa8.2V x9.2.1 x9.2.2 x10.2.0 WP3.2 oa9.2S x10.2.1 x10.2.2
-x11.2.0 oa10.2V x11.2.1 x11.2.2 WP4.2 oa11.2S W10.2 W11.2
-"""
+H0, H1, C = 0, 1, 2
+PASSES = (H0, H1, C)
 
 
 def tile_diagonal_bfgs_left_s2_kernel(tc, u, v, w, steps, rho, yh, out):
     nc = tc.nc
-    u_rows = u.rearrange("(p i) k -> p i k", i=TILES)
-    st_rows = steps.rearrange("(p i) k -> p i k", i=TILES)
-    out_rows = out.rearrange("(p i) n -> p i n", i=TILES)
+    u_rows = u.rearrange("(p t) k -> p t k", t=TILES)
+    steps_rows = steps.rearrange("(p t) k -> p t k", t=TILES)
+    out_rows = out.rearrange("(p t) n -> p t n", t=TILES)
     v_rows = v.rearrange("(g p j) n -> g p j n", p=P, j=PACK)
-    yh_rows = yh.rearrange("(p j) n -> p j n", j=PACK)
+    right_rows = {H0: v_rows[0], H1: v_rows[1], C: yh.rearrange("(p j) n -> p j n", j=PACK)}
 
     with ExitStack() as ctx:
         keep = ctx.enter_context(tc.tile_pool(name="keep", bufs=1))
-        work = ctx.enter_context(tc.tile_pool(name="work", bufs=3))
-        outs = ctx.enter_context(tc.tile_pool(name="outs", bufs=12))
+        work = ctx.enter_context(tc.tile_pool(name="work", bufs=4))
+        results = ctx.enter_context(tc.tile_pool(name="results", bufs=12))
         psum_t = ctx.enter_context(tc.psum_pool(name="psum_t", bufs=4))
         psum_m = ctx.enter_context(tc.psum_pool(name="psum_m", bufs=4))
         ctx.enter_context(tc.manual_schedule())
 
         w_sb = keep.tile([P, 2, PACK], BF16, name="w_sb")
         rho_sb = keep.tile([P, PACK], BF16, name="rho_sb")
-        neg_rho = keep.tile([P, PACK], BF16, name="neg_rho")
+        minus_rho = keep.tile([P, PACK], BF16, name="minus_rho")
         ident = keep.tile([P, P], F32, name="ident")
-        nc.scalar.dma_start(out=w_sb[:], in_=w.rearrange("(g p j) -> p g j", p=P, j=PACK))
-        nc.scalar.dma_start(out=rho_sb[:], in_=rho.rearrange("(p j) -> p j", j=PACK))
-        make_identity(nc, ident[:])
+        factors = {H0: w_sb[:, 0, :], H1: w_sb[:, 1, :], C: minus_rho[:]}
 
-        raw, u_raw, st_raw, words_u, words_st = {}, {}, {}, {}, {}
-        scaled, grouped, codes, scales = {}, {}, {}, {}
-        xt, gu, gs, ucodes, uscales, scodes, sscales = {}, {}, {}, {}, {}, {}, {}
-        acc, result = {}, {}
-
-        def copy_to(engine, dst, src):
-            if engine == "V":
+        def copy(engine, dst, src):
+            if engine == "vector":
                 nc.vector.tensor_copy(out=dst, in_=src)
             else:
                 nc.scalar.copy(out=dst, in_=src)
 
-        def load(kind, arg):
-            if kind == "u":
-                i = int(arg)
-                t = keep.tile([P, 2, K], BF16, name="u%d" % i)
-                nc.sync.dma_start(out=t[:], in_=u_rows[:, 2 * i : 2 * i + 2, :])
-                for a in (0, 1):
-                    u_raw[2 * i + a] = t[:, a, :].bitcast(F32)
-            elif kind == "s":
-                i = int(arg)
-                t = keep.tile([P, 2, Q], BF16, name="st%d" % i)
-                nc.sync.dma_start(out=t[:], in_=st_rows[:, 2 * i : 2 * i + 2, :])
-                for a in (0, 1):
-                    st_raw[2 * i + a] = t[:, a, :].bitcast(F32)
-            else:
-                b, c = int(arg[0]), int(arg[1:] or 1)
-                width = CH if kind == "b" else 2 * CH
-                t = keep.tile([P, PACK, width], BF16, name="raw%d_%d" % (b, c))
-                src = yh_rows if b == 2 else v_rows[b]
-                nc.sync.dma_start(out=t[:], in_=src[:, :, c * CH : c * CH + width])
-                for d in range(width // CH):
-                    raw[b, c + d] = t[:, :, d * CH : (d + 1) * CH]
+        def quantize(grouped, columns, name, dtype):
+            codes = keep.tile([P, columns], U32, name="codes_" + name, align_bytes=64)
+            scales = keep.tile([P, columns], U8, name="scales_" + name, align_bytes=64)
+            nc.vector.quantize_mx(out=codes[:].bitcast(dtype), scales=scales[:], in_=grouped)
+            return codes, scales
 
-        def perm_u(t):
-            x = work.tile([P, 2, 2, P], F32, name="uperm", bufs=3)
-            nc.vector.tensor_copy(out=x[:], in_=u_raw[t].rearrange("p (g r h) -> p g h r", g=2, h=2))
-            words_u[t] = x
+        raw, scaled, grouped_right, right = {}, {}, {}, {}
 
-        def perm_s(t):
-            x = work.tile([P, 2, P], F32, name="sperm", bufs=3)
-            nc.vector.tensor_copy(out=x[:], in_=st_raw[t].rearrange("p (r h) -> p h r", h=2))
-            words_st[t] = x
-
-        def tr_u(t):
-            x = psum_t.tile([P, 4, P], F32, name="xt")
-            for g in (0, 1):
-                for h in (0, 1):
-                    if t in words_u:
-                        src = words_u[t][:, g, h, :]
-                    else:
-                        src = u_raw[t][:, 256 * g + h : 256 * (g + 1) : 2]
-                    nc.tensor.transpose(x[:, 2 * g + h, :], src, ident[:])
-            xt["u", t] = x
-
-        def tr_s(t):
-            i, a = divmod(t, 2)
-            if ("s", i) not in xt:
-                xt["s", i] = psum_t.tile([P, 4, P], F32, name="xt")
-            for h in (0, 1):
-                src = words_st[t][:, h, :] if t in words_st else st_raw[t][:, h:256:2]
-                nc.tensor.transpose(xt["s", i][:, 2 * a + h, :], src, ident[:])
-
-        def out_u(t, engine):
-            gu[t] = work.tile([P, 2 * P * PACK], BF16, name="gu", align_bytes=64, bufs=4)
-            copy_to(
-                engine,
-                gu[t][:].bitcast(F32).rearrange("p (g r h) -> p g r h", g=2, h=2),
-                xt["u", t][:].rearrange("p (g h) r -> p g r h", h=2),
+        def load_right(b, c, chunks=1):
+            tile = keep.tile([P, PACK, chunks * CHUNK], BF16, name="raw_%d_%d" % (b, c))
+            nc.sync.dma_start(
+                out=tile[:], in_=right_rows[b][:, :, c * CHUNK : (c + chunks) * CHUNK]
             )
+            for d in range(chunks):
+                raw[b, c + d] = tile[:, :, d * CHUNK : (d + 1) * CHUNK]
 
-        def out_s(i, engine):
-            gs[i] = work.tile([P, 2 * P * PACK], BF16, name="gs", align_bytes=64)
-            copy_to(
-                engine,
-                gs[i][:].bitcast(F32).rearrange("p (a r h) -> p a r h", a=2, h=2),
-                xt["s", i][:].rearrange("p (a h) r -> p a r h", h=2),
-            )
-
-        def quant_u(t):
-            ucodes[t] = keep.tile([P, 2 * P], U32, name="uc%d" % t, align_bytes=64)
-            uscales[t] = keep.tile([P, 2 * P], U8, name="us%d" % t, align_bytes=64)
-            nc.vector.quantize_mx(out=ucodes[t][:].bitcast(E4M3), scales=uscales[t][:], in_=gu[t][:])
-
-        def quant_s(i):
-            scodes[i] = keep.tile([P, 2 * P], U32, name="sc%d" % i, align_bytes=64)
-            sscales[i] = keep.tile([P, 2 * P], U8, name="ss%d" % i, align_bytes=64)
-            nc.vector.quantize_mx(out=scodes[i][:].bitcast(E4M3), scales=sscales[i][:], in_=gs[i][:])
-
-        def mul(b, c):
-            if b == 2 and c == 0:
-                nc.vector.tensor_scalar(
-                    out=neg_rho[:], in0=rho_sb[:], scalar1=-1.0, scalar2=None, op0=MULT
-                )
-            t = work.tile([P, PACK, CH], BF16, name="scaled", bufs=4)
+        def scale_right(b, c):
+            scaled[b, c] = work.tile([P, PACK, CHUNK], BF16, name="scaled")
             for j in range(PACK):
-                factor = neg_rho[:, j : j + 1] if b == 2 else w_sb[:, b, j : j + 1]
                 nc.vector.tensor_scalar(
-                    out=t[:, j, :], in0=raw[b, c][:, j, :], scalar1=factor, scalar2=None, op0=MULT
+                    out=scaled[b, c][:, j, :],
+                    in0=raw[b, c][:, j, :],
+                    scalar1=factors[b][:, j : j + 1],
+                    scalar2=None,
+                    op0=MULT,
                 )
-            scaled[b, c] = t
 
-        def interleave(b, c, h, engine):
-            if (b, c) not in grouped:
-                grouped[b, c] = work.tile([P, CH, PACK], BF16, name="grouped", align_bytes=64, bufs=4)
-            cols = slice(HALF * h, HALF * (h + 1))
-            copy_to(
+        def interleave_right(b, c, second_half="vector"):
+            grouped_right[b, c] = work.tile([P, CHUNK, PACK], BF16, name="grouped", align_bytes=64)
+            for engine, first in (("vector", 0), (second_half, HALF)):
+                cols = slice(first, first + HALF)
+                copy(
+                    engine,
+                    grouped_right[b, c][:, cols, :].rearrange("p (n i) j -> p n j i", i=4),
+                    scaled[b, c][:, :, cols].rearrange("p j (n i) -> p n j i", i=4),
+                )
+
+        def quantize_right(b, c):
+            right[b, c] = quantize(
+                grouped_right[b, c][:].rearrange("p n j -> p (n j)"),
+                CHUNK,
+                "right_%d_%d" % (b, c),
+                E5M2 if b == C else E4M3,
+            )
+
+        u_pairs, steps_pairs = {}, {}
+        bank, grouped_left, left = {}, {}, {}
+
+        def load_left(rows, width, pairs, t, count):
+            tile = keep.tile([P, count, width], BF16, name="left_%d_%d" % (width, t))
+            nc.sync.dma_start(out=tile[:], in_=rows[:, t : t + count, :])
+            for a in range(count):
+                pairs[t + a] = tile[:, a, :].bitcast(F32)
+
+        def load_u(t, count):
+            load_left(u_rows, K, u_pairs, t, count)
+
+        def load_steps(t, count):
+            load_left(steps_rows, Q, steps_pairs, t, count)
+
+        def transpose_pass(key, slot, pairs, g):
+            for h in (0, 1):
+                nc.tensor.transpose(
+                    bank[key][:, 2 * slot + h, :],
+                    pairs[:, PAIRS_PASS * g + h : PAIRS_PASS * (g + 1) : 2],
+                    ident[:],
+                )
+
+        def transpose_u(t):
+            bank["u", t] = psum_t.tile([P, 4, P], F32, name="bank")
+            for g in (0, 1):
+                transpose_pass(("u", t), g, u_pairs[t], g)
+
+        def transpose_steps(i):
+            bank["steps", i] = psum_t.tile([P, 4, P], F32, name="bank")
+            for a in (0, 1):
+                transpose_pass(("steps", i), a, steps_pairs[2 * i + a], 0)
+
+        def copy_out(key, engine):
+            grouped_left[key] = work.tile(
+                [P, 2 * P * PACK], BF16, name="grouped_left", align_bytes=64, bufs=6
+            )
+            copy(
                 engine,
-                grouped[b, c][:, cols, :].rearrange("p (c i) t -> p c t i", i=4),
-                scaled[b, c][:, :, cols].rearrange("p t (c i) -> p c t i", i=4),
+                grouped_left[key][:].bitcast(F32).rearrange("p (s r h) -> p s r h", s=2, h=2),
+                bank[key][:].rearrange("p (s h) r -> p s r h", h=2),
             )
 
-        def quant(b, c):
-            codes[b, c] = keep.tile([P, CH], U32, name="vc%d_%d" % (b, c), align_bytes=64)
-            scales[b, c] = keep.tile([P, CH], U8, name="vs%d_%d" % (b, c), align_bytes=64)
-            nc.vector.quantize_mx(
-                out=codes[b, c][:].bitcast(E5M2 if b == 2 else E4M3),
-                scales=scales[b, c][:],
-                in_=grouped[b, c][:].rearrange("p c t -> p (c t)"),
-            )
+        def quantize_left(key):
+            left[key] = quantize(grouped_left[key][:], 2 * P, "%s_%d" % key, E4M3)
 
-        def mx(t, c, b):
-            if b == 0:
-                acc[t, c] = psum_m.tile([P, CH], F32, name="acc")
-            if b == 2:
-                i, s = divmod(t, 2)
-                lhs, lsc = scodes[i], sscales[i]
-            else:
-                lhs, lsc, s = ucodes[t], uscales[t], b
+        acc, result = {}, {}
+
+        def multiply(t, c, b):
+            if b == H0:
+                acc[t, c] = psum_m.tile([P, CHUNK], F32, name="acc")
+            key, slot = (("steps", t // 2), t % 2) if b == C else (("u", t), b)
+            cols = slice(slot * P, (slot + 1) * P)
             nc.tensor.matmul_mx(
                 out=acc[t, c][:],
-                lhsT=lhs[:, s * P : (s + 1) * P].bitcast(E4M3),
-                lhsT_scale=lsc[:, s * P : (s + 1) * P],
-                rhs=codes[b, c][:].bitcast(E5M2 if b == 2 else E4M3),
-                rhs_scale=scales[b, c][:],
-                start=(b == 0),
-                stop=(b == 2),
+                lhsT=left[key][0][:, cols].bitcast(E4M3),
+                lhsT_scale=left[key][1][:, cols],
+                rhs=right[b, c][0][:].bitcast(E5M2 if b == C else E4M3),
+                rhs_scale=right[b, c][1][:],
+                start=(b == H0),
+                stop=(b == C),
             )
 
-        def result_of(t, c):
-            if (t // 2, c) not in result:
-                result[t // 2, c] = outs.tile([P, 2, CH], F32, name="result")
-            return result[t // 2, c][:, t % 2, :]
+        def empty(t, c, engine):
+            i, a = divmod(t, 2)
+            if a == 0:
+                result[i, c] = results.tile([P, 2, CHUNK], F32, name="result")
+            copy(engine, result[i, c][:, a, :], acc[t, c][:])
 
-        def out_acc(t, c, engine):
-            dst = result_of(t, c)
-            if (t, c) == LAST:
-                for h, e in ((0, "V"), (1, "S")):
-                    cols = slice(HALF * h, HALF * (h + 1))
-                    copy_to(e, dst[:, cols], acc[t, c][:, cols])
-            else:
-                copy_to(engine, dst, acc[t, c][:])
-
-        def store(t, c):
-            for cols in (slice(0, HALF), slice(HALF, CH)) if (t, c) == LAST else (slice(0, CH),):
-                nc.sync.dma_start(
-                    out=out_rows[:, t, c * CH + cols.start : c * CH + cols.stop], in_=result_of(t, c)[:, cols]
-                )
-
-        def store_pair(i, c):
+        def store(i, c):
             nc.sync.dma_start(
-                out=out_rows[:, 2 * i : 2 * i + 2, c * CH : (c + 1) * CH], in_=result[i, c][:]
+                out=out_rows[:, 2 * i : 2 * i + 2, c * CHUNK : (c + 1) * CHUNK],
+                in_=result[i, c][:],
             )
 
-        LAST = (11, 2)
-        for step in SCHEDULE.split():
-            if step[:1] == "L":
-                load(step[1:2], step[2:])
-            elif step[:2] == "WP":
-                store_pair(*[int(x) for x in step[2:].split(".")])
-            elif step[:1] == "W":
-                store(*[int(x) for x in step[1:].split(".")])
-            elif step[:2] == "pu":
-                perm_u(int(step[2:]))
-            elif step[:2] == "ps":
-                perm_s(int(step[2:]))
-            elif step[:2] == "tu":
-                tr_u(int(step[2:]))
-            elif step[:2] == "ts":
-                tr_s(int(step[2:]))
-            elif step[:2] == "ou":
-                out_u(int(step[2:-1]), step[-1:])
-            elif step[:2] == "os":
-                out_s(int(step[2:-1]), step[-1:])
-            elif step[:2] == "qu":
-                quant_u(int(step[2:]))
-            elif step[:2] == "qs":
-                quant_s(int(step[2:]))
-            elif step[:1] == "m":
-                mul(int(step[1:2]), int(step[2:]))
-            elif step[:1] == "i":
-                interleave(int(step[1:2]), int(step[2:3]), int(step[3:4]), step[4:])
-            elif step[:1] == "q":
-                quant(int(step[1:2]), int(step[2:]))
-            elif step[:1] == "x":
-                mx(*[int(x) for x in step[1:].split(".")])
-            else:
-                t, c = step[2:-1].split(".")
-                out_acc(int(t), int(c), step[-1:])
+        nc.scalar.dma_start(out=w_sb[:], in_=w.rearrange("(g p j) -> p g j", p=P, j=PACK))
+        make_identity(nc, ident[:])
+        load_right(H0, 0)
+        load_u(0, 2)
+        load_u(2, 2)
+        load_right(H1, 0)
+        nc.sync.dma_start(out=rho_sb[:], in_=rho.rearrange("(p j) -> p j", j=PACK))
+        load_steps(0, 4)
+        load_u(4, 2)
+        load_steps(4, 4)
+        load_right(C, 0)
+        load_u(6, 2)
+        load_steps(8, 4)
+        load_u(8, 4)
+        load_right(H0, 1)
+        load_right(H1, 1)
+        load_right(C, 1, chunks=2)
+        load_right(H0, 2)
+        load_right(H1, 2)
+
+        scale_right(H0, 0)
+        interleave_right(H0, 0)
+        for t in range(4):
+            transpose_u(t)
+        for t in range(3):
+            copy_out(("u", t), "scalar")
+        quantize_right(H0, 0)
+        quantize_left(("u", 0))
+        quantize_left(("u", 1))
+        copy_out(("u", 3), "vector")
+        quantize_left(("u", 2))
+        quantize_left(("u", 3))
+        for t in range(3):
+            multiply(t, 0, H0)
+
+        scale_right(H1, 0)
+        interleave_right(H1, 0)
+        for i in (0, 1):
+            transpose_steps(i)
+            copy_out(("steps", i), "scalar")
+        for t in (4, 5):
+            transpose_u(t)
+            copy_out(("u", t), "scalar")
+        for i in (2, 3):
+            transpose_steps(i)
+            copy_out(("steps", i), "scalar")
+        quantize_left(("steps", 0))
+        quantize_right(H1, 0)
+        quantize_left(("steps", 1))
+        multiply(3, 0, H0)
+        for t in range(4):
+            multiply(t, 0, H1)
+
+        quantize_left(("u", 4))
+        quantize_left(("u", 5))
+        nc.vector.tensor_scalar(
+            out=minus_rho[:], in0=rho_sb[:], scalar1=-1.0, scalar2=None, op0=MULT
+        )
+        scale_right(C, 0)
+        quantize_left(("steps", 2))
+        interleave_right(C, 0)
+        quantize_left(("steps", 3))
+        quantize_right(C, 0)
+        for t in (6, 7):
+            transpose_u(t)
+            copy_out(("u", t), "scalar")
+            quantize_left(("u", t))
+        for i in (4, 5):
+            transpose_steps(i)
+            copy_out(("steps", i), "scalar")
+        quantize_left(("steps", 4))
+        for t in range(4):
+            multiply(t, 0, C)
+            empty(t, 0, "vector" if t == 3 else "scalar")
+            if t % 2:
+                store(t // 2, 0)
+        quantize_left(("steps", 5))
+
+        for t in range(8, 12):
+            transpose_u(t)
+            copy_out(("u", t), "vector" if t == 8 else "scalar")
+        scale_right(H0, 1)
+        for t in (8, 9, 10):
+            quantize_left(("u", t))
+        interleave_right(H0, 1, second_half="scalar")
+        quantize_left(("u", 11))
+
+        def multiply_pair(t, first_engine):
+            for b in PASSES:
+                multiply(t, 0, b)
+                multiply(t + 1, 0, b)
+            empty(t, 0, first_engine)
+            empty(t + 1, 0, "scalar")
+            store(t // 2, 0)
+
+        multiply_pair(4, "vector")
+        quantize_right(H0, 1)
+        scale_right(H1, 1)
+        scale_right(C, 1)
+        multiply_pair(6, "scalar")
+        interleave_right(H1, 1, second_half="scalar")
+        interleave_right(C, 1, second_half="scalar")
+        multiply_pair(8, "vector")
+        quantize_right(H1, 1)
+        multiply_pair(10, "vector")
+        quantize_right(C, 1)
+
+        for t in range(3):
+            multiply(t, 1, H0)
+            multiply(t, 1, H1)
+        for t in range(TILES):
+            for b in PASSES if t >= 3 else (C,):
+                multiply(t, 1, b)
+            empty(t, 1, "scalar")
+            if t % 2:
+                store(t // 2, 1)
+        scale_right(C, 2)
+        scale_right(H0, 2)
+        interleave_right(C, 2)
+        scale_right(H1, 2)
+        interleave_right(H0, 2)
+        quantize_right(C, 2)
+        interleave_right(H1, 2)
+        quantize_right(H0, 2)
+        quantize_right(H1, 2)
+
+        last = TILES - 1
+        for t in range(last):
+            for b in PASSES:
+                multiply(t, 2, b)
+            empty(t, 2, "vector" if t % 2 else "scalar")
+            if t % 2:
+                store(t // 2, 2)
+        nc.sync.dma_start(out=out_rows[:, last - 1, 2 * CHUNK :], in_=result[last // 2, 2][:, 0, :])
+        for b in PASSES:
+            multiply(last, 2, b)
+        for engine, first in (("vector", 0), ("scalar", HALF)):
+            part = result[last // 2, 2][:, 1, first : first + HALF]
+            copy(engine, part, acc[last, 2][:, first : first + HALF])
+            nc.sync.dma_start(
+                out=out_rows[:, last, 2 * CHUNK + first : 2 * CHUNK + first + HALF], in_=part
+            )

from contextlib import ExitStack

import concourse.mybir as mybir
from concourse.masks import make_identity

N, K, Q = 1536, 1024, 512
FLOPS = 2 * N * N * (K + Q)

F32 = mybir.dt.float32
BF16 = mybir.dt.bfloat16
U32 = mybir.dt.uint32
U8 = mybir.dt.uint8
E4M3 = mybir.dt.float8_e4m3fn_x4
E5M2 = mybir.dt.float8_e5m2_x4
MULT = mybir.AluOpType.mult

P = 128
PACK = 4
PAIRS_PASS = 2 * P
TILES = N // P
CHUNK = 512
HALF = CHUNK // 2

H0, H1, C = 0, 1, 2
PASSES = (H0, H1, C)


def tile_diagonal_bfgs_left_s2_kernel(tc, u, v, w, steps, rho, yh, out):
    nc = tc.nc
    u_rows = u.rearrange("(p t) k -> p t k", t=TILES)
    steps_rows = steps.rearrange("(p t) k -> p t k", t=TILES)
    out_rows = out.rearrange("(p t) n -> p t n", t=TILES)
    v_rows = v.rearrange("(g p j) n -> g p j n", p=P, j=PACK)
    right_rows = {H0: v_rows[0], H1: v_rows[1], C: yh.rearrange("(p j) n -> p j n", j=PACK)}

    with ExitStack() as ctx:
        keep = ctx.enter_context(tc.tile_pool(name="keep", bufs=1))
        work = ctx.enter_context(tc.tile_pool(name="work", bufs=4))
        results = ctx.enter_context(tc.tile_pool(name="results", bufs=12))
        psum_t = ctx.enter_context(tc.psum_pool(name="psum_t", bufs=4))
        psum_m = ctx.enter_context(tc.psum_pool(name="psum_m", bufs=4))
        ctx.enter_context(tc.manual_schedule())

        w_sb = keep.tile([P, 2, PACK], BF16, name="w_sb")
        rho_sb = keep.tile([P, PACK], BF16, name="rho_sb")
        minus_rho = keep.tile([P, PACK], BF16, name="minus_rho")
        ident = keep.tile([P, P], F32, name="ident")
        factors = {H0: w_sb[:, 0, :], H1: w_sb[:, 1, :], C: minus_rho[:]}

        def copy(engine, dst, src):
            if engine == "vector":
                nc.vector.tensor_copy(out=dst, in_=src)
            else:
                nc.scalar.copy(out=dst, in_=src)

        def quantize(grouped, columns, name, dtype):
            codes = keep.tile([P, columns], U32, name="codes_" + name, align_bytes=64)
            scales = keep.tile([P, columns], U8, name="scales_" + name, align_bytes=64)
            nc.vector.quantize_mx(out=codes[:].bitcast(dtype), scales=scales[:], in_=grouped)
            return codes, scales

        raw, scaled, grouped_right, right = {}, {}, {}, {}

        def load_right(b, c, chunks=1):
            tile = keep.tile([P, PACK, chunks * CHUNK], BF16, name="raw_%d_%d" % (b, c))
            nc.sync.dma_start(
                out=tile[:], in_=right_rows[b][:, :, c * CHUNK : (c + chunks) * CHUNK]
            )
            for d in range(chunks):
                raw[b, c + d] = tile[:, :, d * CHUNK : (d + 1) * CHUNK]

        def scale_right(b, c):
            scaled[b, c] = work.tile([P, PACK, CHUNK], BF16, name="scaled")
            for j in range(PACK):
                nc.vector.tensor_scalar(
                    out=scaled[b, c][:, j, :],
                    in0=raw[b, c][:, j, :],
                    scalar1=factors[b][:, j : j + 1],
                    scalar2=None,
                    op0=MULT,
                )

        def interleave_right(b, c, second_half="vector"):
            grouped_right[b, c] = work.tile([P, CHUNK, PACK], BF16, name="grouped", align_bytes=64)
            for engine, first in (("vector", 0), (second_half, HALF)):
                cols = slice(first, first + HALF)
                copy(
                    engine,
                    grouped_right[b, c][:, cols, :].rearrange("p (n i) j -> p n j i", i=4),
                    scaled[b, c][:, :, cols].rearrange("p j (n i) -> p n j i", i=4),
                )

        def quantize_right(b, c):
            right[b, c] = quantize(
                grouped_right[b, c][:].rearrange("p n j -> p (n j)"),
                CHUNK,
                "right_%d_%d" % (b, c),
                E5M2 if b == C else E4M3,
            )

        u_pairs, steps_pairs = {}, {}
        bank, grouped_left, left = {}, {}, {}

        def load_left(rows, width, pairs, t, count):
            tile = keep.tile([P, count, width], BF16, name="left_%d_%d" % (width, t))
            nc.sync.dma_start(out=tile[:], in_=rows[:, t : t + count, :])
            for a in range(count):
                pairs[t + a] = tile[:, a, :].bitcast(F32)

        def load_u(t, count):
            load_left(u_rows, K, u_pairs, t, count)

        def load_steps(t, count):
            load_left(steps_rows, Q, steps_pairs, t, count)

        def transpose_pass(key, slot, pairs, g):
            for h in (0, 1):
                nc.tensor.transpose(
                    bank[key][:, 2 * slot + h, :],
                    pairs[:, PAIRS_PASS * g + h : PAIRS_PASS * (g + 1) : 2],
                    ident[:],
                )

        def transpose_u(t):
            bank["u", t] = psum_t.tile([P, 4, P], F32, name="bank")
            for g in (0, 1):
                transpose_pass(("u", t), g, u_pairs[t], g)

        def transpose_steps(i):
            bank["steps", i] = psum_t.tile([P, 4, P], F32, name="bank")
            for a in (0, 1):
                transpose_pass(("steps", i), a, steps_pairs[2 * i + a], 0)

        def copy_out(key, engine):
            grouped_left[key] = work.tile(
                [P, 2 * P * PACK], BF16, name="grouped_left", align_bytes=64, bufs=6
            )
            copy(
                engine,
                grouped_left[key][:].bitcast(F32).rearrange("p (s r h) -> p s r h", s=2, h=2),
                bank[key][:].rearrange("p (s h) r -> p s r h", h=2),
            )

        def quantize_left(key):
            left[key] = quantize(grouped_left[key][:], 2 * P, "%s_%d" % key, E4M3)

        acc, result = {}, {}

        def multiply(t, c, b):
            if b == H0:
                acc[t, c] = psum_m.tile([P, CHUNK], F32, name="acc")
            key, slot = (("steps", t // 2), t % 2) if b == C else (("u", t), b)
            cols = slice(slot * P, (slot + 1) * P)
            nc.tensor.matmul_mx(
                out=acc[t, c][:],
                lhsT=left[key][0][:, cols].bitcast(E4M3),
                lhsT_scale=left[key][1][:, cols],
                rhs=right[b, c][0][:].bitcast(E5M2 if b == C else E4M3),
                rhs_scale=right[b, c][1][:],
                start=(b == H0),
                stop=(b == C),
            )

        def empty(t, c, engine):
            i, a = divmod(t, 2)
            if a == 0:
                result[i, c] = results.tile([P, 2, CHUNK], F32, name="result")
            copy(engine, result[i, c][:, a, :], acc[t, c][:])

        def store(i, c):
            nc.sync.dma_start(
                out=out_rows[:, 2 * i : 2 * i + 2, c * CHUNK : (c + 1) * CHUNK],
                in_=result[i, c][:],
            )

        nc.scalar.dma_start(out=w_sb[:], in_=w.rearrange("(g p j) -> p g j", p=P, j=PACK))
        make_identity(nc, ident[:])
        load_right(H0, 0)
        load_u(0, 2)
        load_u(2, 2)
        load_right(H1, 0)
        nc.sync.dma_start(out=rho_sb[:], in_=rho.rearrange("(p j) -> p j", j=PACK))
        load_steps(0, 4)
        load_u(4, 2)
        load_steps(4, 4)
        load_right(C, 0)
        load_u(6, 2)
        load_steps(8, 4)
        load_u(8, 4)
        load_right(H0, 1)
        load_right(H1, 1)
        load_right(C, 1, chunks=2)
        load_right(H0, 2)
        load_right(H1, 2)

        scale_right(H0, 0)
        interleave_right(H0, 0)
        for t in range(4):
            transpose_u(t)
        for t in range(3):
            copy_out(("u", t), "scalar")
        quantize_right(H0, 0)
        quantize_left(("u", 0))
        quantize_left(("u", 1))
        copy_out(("u", 3), "vector")
        quantize_left(("u", 2))
        quantize_left(("u", 3))
        for t in range(3):
            multiply(t, 0, H0)

        scale_right(H1, 0)
        interleave_right(H1, 0)
        for i in (0, 1):
            transpose_steps(i)
            copy_out(("steps", i), "scalar")
        for t in (4, 5):
            transpose_u(t)
            copy_out(("u", t), "scalar")
        for i in (2, 3):
            transpose_steps(i)
            copy_out(("steps", i), "scalar")
        quantize_left(("steps", 0))
        quantize_right(H1, 0)
        quantize_left(("steps", 1))
        multiply(3, 0, H0)
        for t in range(4):
            multiply(t, 0, H1)

        quantize_left(("u", 4))
        quantize_left(("u", 5))
        nc.vector.tensor_scalar(
            out=minus_rho[:], in0=rho_sb[:], scalar1=-1.0, scalar2=None, op0=MULT
        )
        scale_right(C, 0)
        quantize_left(("steps", 2))
        interleave_right(C, 0)
        quantize_left(("steps", 3))
        quantize_right(C, 0)
        for t in (6, 7):
            transpose_u(t)
            copy_out(("u", t), "scalar")
            quantize_left(("u", t))
        for i in (4, 5):
            transpose_steps(i)
            copy_out(("steps", i), "scalar")
        quantize_left(("steps", 4))
        for t in range(4):
            multiply(t, 0, C)
            empty(t, 0, "vector" if t == 3 else "scalar")
            if t % 2:
                store(t // 2, 0)
        quantize_left(("steps", 5))

        for t in range(8, 12):
            transpose_u(t)
            copy_out(("u", t), "vector" if t == 8 else "scalar")
        scale_right(H0, 1)
        for t in (8, 9, 10):
            quantize_left(("u", t))
        interleave_right(H0, 1, second_half="scalar")
        quantize_left(("u", 11))

        def multiply_pair(t, first_engine):
            for b in PASSES:
                multiply(t, 0, b)
                multiply(t + 1, 0, b)
            empty(t, 0, first_engine)
            empty(t + 1, 0, "scalar")
            store(t // 2, 0)

        multiply_pair(4, "vector")
        quantize_right(H0, 1)
        scale_right(H1, 1)
        scale_right(C, 1)
        multiply_pair(6, "scalar")
        interleave_right(H1, 1, second_half="scalar")
        interleave_right(C, 1, second_half="scalar")
        multiply_pair(8, "vector")
        quantize_right(H1, 1)
        multiply_pair(10, "vector")
        quantize_right(C, 1)

        for t in range(3):
            multiply(t, 1, H0)
            multiply(t, 1, H1)
        for t in range(TILES):
            for b in PASSES if t >= 3 else (C,):
                multiply(t, 1, b)
            empty(t, 1, "scalar")
            if t % 2:
                store(t // 2, 1)
        scale_right(C, 2)
        scale_right(H0, 2)
        interleave_right(C, 2)
        scale_right(H1, 2)
        interleave_right(H0, 2)
        quantize_right(C, 2)
        interleave_right(H1, 2)
        quantize_right(H0, 2)
        quantize_right(H1, 2)

        last = TILES - 1
        for t in range(last):
            for b in PASSES:
                multiply(t, 2, b)
            empty(t, 2, "vector" if t % 2 else "scalar")
            if t % 2:
                store(t // 2, 2)
        nc.sync.dma_start(out=out_rows[:, last - 1, 2 * CHUNK :], in_=result[last // 2, 2][:, 0, :])
        for b in PASSES:
            multiply(last, 2, b)
        for engine, first in (("vector", 0), ("scalar", HALF)):
            part = result[last // 2, 2][:, 1, first : first + HALF]
            copy(engine, part, acc[last, 2][:, first : first + HALF])
            nc.sync.dma_start(
                out=out_rows[:, last, 2 * CHUNK + first : 2 * CHUNK + first + HALF], in_=part
            )
